import numpy as np
import ml_dtypes


def mxq(x, axis, fmt="e4m3"):
    dtype, down = {"e4m3": (ml_dtypes.float8_e4m3fn, 7), "e5m2": (ml_dtypes.float8_e5m2, 14)}[fmt]
    v = np.moveaxis(np.asarray(x, np.float32).astype(ml_dtypes.bfloat16).astype(np.float64), axis, -1)
    blocks = v.reshape(v.shape[:-1] + (-1, 32))
    amax = np.abs(blocks).max(-1, keepdims=True)
    byte = np.maximum(np.where(amax > 0, np.frexp(amax)[1] - 1 + 127, 0) - down, 1)
    scale = np.exp2(byte - 127.0)
    codes = (blocks / scale).astype(np.float32).astype(dtype).astype(np.float64)
    return np.moveaxis((codes * scale).reshape(v.shape), -1, axis)


WIDE = False


def mx_kscale(k):
    if not WIDE:
        return np.ones(k)
    levels = np.array([10, -10, 5, -5, 0])
    if k % 512:
        return np.exp2(np.random.permutation(np.resize(levels, k // 32))).repeat(32)
    a = np.empty((k // 512, 16))
    for p in range(k // 512):
        a[p, :8] = np.random.permutation(np.resize(levels, 8))
        for g in range(8):
            far = levels[np.abs(levels - a[p, g]) >= 10]
            a[p, g + 8] = far[np.random.randint(len(far))]
    return np.exp2(a.ravel()).repeat(32)


def f64(x):
    return np.asarray(x).astype(np.float64)


def striped(idx):
    return np.tile(idx.reshape(-1, 16).T, (8, 1)).astype(np.uint16)


def unstriped(offs):
    return offs[:16].T.reshape(-1).astype(np.int64)


E2M1 = np.array([0.0, 0.5, 1.0, 1.5, 2.0, 3.0, 4.0, 6.0, -0.0, -0.5, -1.0, -1.5, -2.0, -3.0, -4.0, -6.0])


def pack_weight(w, fmt):
    k, n = w.shape
    w = f64(np.asarray(w, np.float32).astype(ml_dtypes.bfloat16)).reshape(k // 32, 32, n)
    amax = np.abs(w).max(1)
    if fmt == "e4m3":
        byte = np.frexp(amax)[1] - 1 + 127 - 7
    else:
        mant, ex = np.frexp(amax / 6.0)
        byte = np.where(mant > 0.5, ex, ex - 1) + 127
    byte = np.clip(np.where(amax > 0, byte, 1), 1, 254)
    scaled = (w * np.exp2(127.0 - byte)[:, None, :]).reshape(k, n).astype(np.float32)
    by_word = np.ascontiguousarray(scaled.reshape(k // 512, 128, 4, n).transpose(0, 1, 3, 2))
    if fmt == "e4m3":
        words = by_word.astype(ml_dtypes.float8_e4m3fn).view(np.uint8)
    else:
        c = by_word.astype(ml_dtypes.float4_e2m1fn).view(np.uint8) & 0xF
        words = (c[..., 0::2] | (c[..., 1::2] << 4)).reshape(k // 512, 128, 2 * n)
    return np.ascontiguousarray(words), np.ascontiguousarray(byte.astype(np.uint8).reshape(k // 512, 16, n))


def unpack_weight(words, scales, fmt):
    g, _, n = scales.shape
    words = np.ascontiguousarray(words).reshape(g, 128, n, -1)
    if fmt == "e4m3":
        vals = words.view(ml_dtypes.float8_e4m3fn).astype(np.float64)
    else:
        nib = np.empty((g, 128, n, 4), np.uint8)
        nib[..., 0::2] = words & 0xF
        nib[..., 1::2] = words >> 4
        vals = E2M1[nib]
    vals = vals * np.repeat(np.exp2(scales.astype(np.float64) - 127.0), 8, axis=1)[..., None]
    return vals.transpose(0, 1, 3, 2).reshape(g * 512, n)


def gelu(v):
    return 0.5 * v * (1.0 + np.tanh(np.sqrt(2.0 / np.pi) * (v + 0.044715 * v**3)))


def bf(x):
    return np.asarray(x, np.float32).astype(ml_dtypes.bfloat16)


def planes(Y):
    n, m = Y.shape
    b = f64(bf(Y)).reshape(n // 32, 32, m)
    amax = np.abs(b).max(1)
    byte = np.clip(np.where(amax > 0, np.frexp(amax)[1] - 1 + 127 - 7, 1), 1, 254)
    codes = (b * np.exp2(127.0 - byte)[:, None, :]).reshape(n, m).astype(np.float32).astype(ml_dtypes.float8_e4m3fn).view(np.uint8)
    words = codes.reshape(n // 512, 128, 4, m).transpose(0, 1, 3, 2)
    return np.ascontiguousarray(words), np.ascontiguousarray(byte.astype(np.uint8).reshape(n // 512, 16, m))


K, H, N, T, S, P = 1024, 1024, 512, 2048, 1024, 512

def setup_inputs():
    n = np.random.standard_normal
    sk = mx_kscale(K)[:, None]
    u = mx_kscale(H)[:, None]
    tab_words, tab_scales = pack_weight(n((K, T)) * sk, "e4m3")
    w2_words, w2_scales = pack_weight(0.6 * n((K, H)) / np.sqrt(K) / sk, "e2m1")
    w1 = 0.6 * n((K, H)) / np.sqrt(K) / sk
    w3 = 0.6 * n((H, N)) / np.sqrt(H) / u * np.exp(0.8 * n(N))[None, :]
    mix = np.random.uniform(0.3, 0.8, H) * np.sign(n(H)) * u[:, 0]
    return {
        "tab_words": tab_words, "tab_scales": tab_scales,
        "offs": striped(np.random.permutation(T)[:S]),
        "pos1": striped(np.random.permutation(S)[:P]),
        "pos2": striped(np.random.permutation(S)[:P]),
        "w1": w1.astype(np.float32),
        "w2_words": w2_words, "w2_scales": w2_scales,
        "blank": (0.4 * n(S)).astype(np.float32),
        "temp": np.random.uniform(0.4, 1.6, H).astype(np.float32),
        "shift": (0.5 * n(H)).astype(np.float32),
        "base": np.random.uniform(0.02, 0.05, H).astype(np.float32),
        "mix": mix.astype(np.float32),
        "lattice": (0.6 * n((H, P)) * u).astype(np.float32),
        "w3": w3.astype(np.float32),
    }

def reference(tab_words, tab_scales, offs, pos1, pos2, w1, w2_words, w2_scales,
              blank, temp, shift, base, mix, lattice, w3):
    v = unpack_weight(tab_words, tab_scales, "e4m3")[:, unstriped(offs)]
    w1q = mxq(f64(w1), 0, "e4m3")
    w2 = unpack_weight(w2_words, w2_scales, "e2m1")
    both = np.vstack([(w1q.T @ v), (w2.T @ v)]) - f64(blank)[None, :]
    h, g = both[:H], both[H:]
    top = h.max(axis=1)
    a = np.exp(h[:, unstriped(pos1)] - top[:, None])
    c = np.exp(f64(temp)[:, None] * g[:, unstriped(pos2)] + f64(shift)[:, None])
    z = f64(mix)[:, None] * (np.log(a + f64(base)[:, None]) + c) + f64(lattice)
    zq = mxq(z, 0, "e4m3")
    w3q = mxq(f64(w3), 0, "e4m3")
    y = w3q.T @ zq
    words, scales = planes(y)
    return y, words, scales

@@ -1,0 +1,344 @@
+from contextlib import ExitStack
+
+import concourse.mybir as mybir
+from concourse.masks import make_identity
+
+K, H, N, T, S, M = 1024, 1024, 512, 2048, 1024, 512
+FLOPS = 2 * K * H * S * 2 + 2 * H * N * M
+
+F32 = mybir.dt.float32
+BF16 = mybir.dt.bfloat16
+I32 = mybir.dt.int32
+U32 = mybir.dt.uint32
+U16 = mybir.dt.uint16
+U8 = mybir.dt.uint8
+FP8X4 = mybir.dt.float8_e4m3fn_x4
+FP4X4 = mybir.dt.float4_e2m1fn_x4
+ACT = mybir.ActivationFunctionType
+ALU = mybir.AluOpType
+
+P = 128
+PACK = 4
+PASS = P * PACK
+BANK = 512
+PASSES = K // PASS
+SLICES = H // P
+HALVES = S // BANK
+QUARTER = 128
+
+
+def tile_list_polymorph_well_features_kernel(
+    tc, tab_words, tab_scales, offs, pos1, pos2, w1, w2_words, w2_scales,
+    blank, temp, shift, base, mix, lattice, w3, out_0, out_1, out_2,
+):
+    nc = tc.nc
+    with ExitStack() as ctx:
+        lists = ctx.enter_context(tc.tile_pool(name="lists", bufs=1))
+        keep = ctx.enter_context(tc.tile_pool(name="keep", bufs=1))
+        raw = ctx.enter_context(tc.tile_pool(name="raw", bufs=4))
+        scores = ctx.enter_context(tc.tile_pool(name="scores", bufs=8))
+        psum = ctx.enter_context(tc.psum_pool(name="psum", bufs=8))
+
+        def held(shape, dtype, name, tag=""):
+            return keep.tile(shape, dtype, name=name, tag=tag or name, align_bytes=64)
+
+        offs_t = lists.tile([P, S // 16], U16, name="offs_t")
+        pos1_t = lists.tile([P, M // 16], U16, name="pos1_t")
+        pos2_t = lists.tile([P, M // 16], U16, name="pos2_t")
+
+        tab_s = held([P, PASSES, T], U8, "tab_s")
+        w2_s_raw = held([P, PASSES, H], U8, "w2_s_raw")
+        nc.gpsimd.memset(tab_s[:, 0, :].bitcast(I32), 0)
+        nc.vector.memset(tab_s[:, 1, :].bitcast(I32), 0)
+        nc.vector.memset(w2_s_raw[:].bitcast(I32), 0)
+        ident = held([P, P], F32, "ident")
+        make_identity(nc, ident[:])
+
+        nc.sync.dma_start(offs_t[:], offs)
+        blank_col = held([P, S // P], F32, "blank_col")
+        nc.sync.dma_start(out=blank_col[:], in_=blank.rearrange("(p c) -> p c", p=P))
+        tab_w = [held([P, T], U32, "tab_w%d" % a) for a in range(PASSES)]
+
+        def load_table_words(a):
+            nc.sync.dma_start(
+                out=tab_w[a][:].bitcast(I32),
+                in_=tab_words[a].rearrange("p n t -> p (n t)").bitcast(I32),
+            )
+
+        load_table_words(0)
+        for q in range(4):
+            nc.scalar.dma_start(
+                out=tab_s[32 * q : 32 * q + 4, :, :].bitcast(I32),
+                in_=tab_scales[:, 4 * q : 4 * q + 4, :].rearrange("a r e -> r a e").bitcast(I32),
+            )
+        load_table_words(1)
+        w2_raw = held([P, PASSES, 2 * H], U8, "w2_raw")
+        nc.sync.dma_start(
+            out=w2_raw[:].bitcast(I32), in_=w2_words.rearrange("a p e -> p a e").bitcast(I32)
+        )
+        for q in range(4):
+            nc.sync.dma_start(
+                out=w2_s_raw[32 * q : 32 * q + 4, :, :].bitcast(I32),
+                in_=w2_scales[:, 4 * q : 4 * q + 4, :].rearrange("a r e -> r a e").bitcast(I32),
+            )
+
+        def load_rows(vec, name):
+            cols = held([P, SLICES], F32, name)
+            nc.sync.dma_start(
+                out=cols[:].rearrange("p (b t) -> p b t", t=PACK),
+                in_=vec.rearrange("(b p t) -> p b t", p=P, t=PACK),
+            )
+            return cols
+
+        def load_weight(w, a, b, chunk=None):
+            if chunk is None:
+                chunk = raw.tile([P, PACK, PASS], F32, name="w_raw", tag="w_raw")
+            nc.sync.dma_start(
+                out=chunk[:],
+                in_=w[a * PASS : (a + 1) * PASS, b * PASS : (b + 1) * PASS].rearrange(
+                    "(p i) c -> p i c", i=PACK
+                ),
+            )
+            return chunk
+
+        w1_raw = {}
+        w1_raw[0, 0] = load_weight(w1, 0, 0)
+        nc.sync.dma_start(pos2_t[:], pos2)
+        temp_c = load_rows(temp, "temp_c")
+        shift_c = load_rows(shift, "shift_c")
+        w1_raw[1, 0] = load_weight(w1, 1, 0)
+        w1_raw[0, 1] = load_weight(w1, 0, 1)
+        w1_raw[1, 1] = load_weight(w1, 1, 1)
+        nc.sync.dma_start(pos1_t[:], pos1)
+        mix_c = load_rows(mix, "mix_c")
+        base_c = load_rows(base, "base_c")
+
+        blank_all = held([P, S], F32, "blank_all")
+        per_part = S // P
+        for half in range(per_part // 4):
+            spread = psum.tile([P, 4, P], F32, name="spread", tag="acc")
+            for c in range(4):
+                col = 4 * half + c
+                nc.tensor.transpose(
+                    spread[:, c, :], blank_col[:, col : col + 1].to_broadcast([P, P]), ident[:]
+                )
+            nc.scalar.activation(
+                out=blank_all[:].rearrange("p (n c) -> p n c", c=per_part)[:, :, 4 * half : 4 * half + 4],
+                in_=spread[:].rearrange("p c n -> p n c"),
+                func=ACT.Copy,
+            )
+
+        v_s = []
+        for a in range(PASSES):
+            picked = held([P, S], U8, "v_s%d" % a)
+            nc.vector.tensor_copy(picked[:], tab_s[:, a, :].indirect(offs_t[:]))
+            v_s.append(picked)
+
+        w2_w = []
+        for a in range(PASSES):
+            dealt = held([P, 2 * H], U8, "w2_w%d" % a)
+            nc.scalar.copy(
+                out=dealt[:].bitcast(U16).rearrange("p (b t c i) -> p b c t i", t=PACK, c=16, i=8),
+                in_=w2_raw[:, a, :].bitcast(U16).rearrange("p (b c i t) -> p b c t i", t=PACK, c=16, i=8),
+            )
+            w2_w.append(dealt)
+
+        v_w = {}
+        cols_per_half = BANK // 16
+        for a in range(PASSES):
+            for half in range(HALVES):
+                picked = held([P, BANK], U32, "v_w%d%d" % (a, half))
+                nc.vector.tensor_copy(
+                    picked[:],
+                    tab_w[a][:].indirect(offs_t[:, half * cols_per_half : (half + 1) * cols_per_half]),
+                )
+                v_w[a, half] = picked
+
+        w2_s = held([P, PASSES, H], U8, "w2_s")
+        nc.vector.tensor_copy(
+            out=w2_s[:].rearrange("p a (b t c i) -> p (a b) c t i", t=PACK, c=8, i=16),
+            in_=w2_s_raw[:].rearrange("p a (b c i t) -> p (a b) c t i", t=PACK, c=8, i=16),
+        )
+        w3_raw = [
+            load_weight(w3, b, 0, held([P, PACK, N], F32, "w3_raw%d" % b, "tab_w%d" % b))
+            for b in range(H // PASS)
+        ]
+        lat = []
+        for b in range(H // PASS):
+            rows = held([P, PACK, M], F32, "lat%d" % b)
+            nc.sync.dma_start(
+                out=rows[:],
+                in_=lattice[b * PASS : (b + 1) * PASS, :].rearrange("(p t) m -> p t m", t=PACK),
+            )
+            lat.append(rows)
+
+        def round_weight(engine, chunk, name, pieces):
+            rounded = held([P, PACK, P, PACK], BF16, name)
+            step = P // pieces
+            for k in range(pieces):
+                dst = rounded[:, :, k * step : (k + 1) * step, :].rearrange("p t c i -> p c t i")
+                src = chunk[:].rearrange("p i (c t) -> p c t i", t=PACK)[:, k * step : (k + 1) * step, :, :]
+                if engine == "scalar":
+                    nc.scalar.copy(out=dst, in_=src)
+                else:
+                    nc.gpsimd.tensor_scalar(dst, src, 1.0, 0.0, ALU.mult, ALU.add)
+            return rounded
+
+        def quantise(rounded, name):
+            words = held([P, PASS], U32, name + "_w")
+            scales = held([P, PASS], U8, name + "_s")
+            nc.vector.quantize_mx(
+                out=words[:].bitcast(FP8X4),
+                scales=scales[:],
+                in_=rounded[:].rearrange("p t c i -> p (t c i)"),
+            )
+            return words, scales
+
+        w1_q = {}
+        for b in range(H // PASS):
+            for a in range(PASSES):
+                rounded = round_weight("scalar", w1_raw[a, b], "w1_b%d%d" % (a, b), 1)
+                w1_q[a, b] = quantise(rounded, "w1_q%d%d" % (a, b))
+
+        def score(stationary):
+            rows = scores.tile([P, S], F32, name="rows", tag="rows")
+            for half in range(HALVES):
+                cols = slice(half * BANK, (half + 1) * BANK)
+                acc = psum.tile([P, BANK], F32, name="acc", tag="acc")
+                for a in range(PASSES):
+                    words, scales = stationary(a)
+                    nc.tensor.matmul_mx(
+                        out=acc[:],
+                        lhsT=words,
+                        lhsT_scale=scales,
+                        rhs=v_w[a, half][:].bitcast(FP8X4),
+                        rhs_scale=v_s[a][:, cols],
+                        start=(a == 0),
+                        stop=(a == PASSES - 1),
+                    )
+                nc.vector.tensor_tensor(rows[:, cols], acc[:], blank_all[:, cols], ALU.subtract)
+            return rows
+
+        anti = []
+        for s in range(SLICES):
+            g = score(
+                lambda a: (
+                    w2_w[a][:, 2 * P * s : 2 * P * (s + 1)].bitcast(FP4X4),
+                    w2_s[:, a, P * s : P * (s + 1)],
+                )
+            )
+            c = held([P, M], F32, "anti%d" % s)
+            nc.scalar.activation(
+                out=c[:], in_=g[:].indirect(pos2_t[:]), func=ACT.Exp,
+                bias=shift_c[:, s : s + 1], scale=temp_c[:, s : s + 1],
+            )
+            anti.append(c)
+
+        w3_rounded = [round_weight("gpsimd", w3_raw[b], "w3_b%d" % b, 2) for b in range(H // PASS)]
+        for t in range(PACK):
+            nc.gpsimd.tensor_scalar(anti[t][:], anti[t][:], mix_c[:, t : t + 1], 0.0, ALU.mult, ALU.add)
+            nc.gpsimd.tensor_tensor(lat[0][:, t, :], lat[0][:, t, :], anti[t][:], ALU.add)
+
+        neg_top = keep.tile([P, SLICES], F32, name="neg_top", tag="top_then_log", align_bytes=64)
+        cooled = []
+        for s in range(SLICES):
+            b, t = divmod(s, PACK)
+            h = score(
+                lambda a: (
+                    w1_q[a, b][0][:, P * t : P * (t + 1)].bitcast(FP8X4),
+                    w1_q[a, b][1][:, P * t : P * (t + 1)],
+                )
+            )
+            nc.vector.tensor_reduce(
+                neg_top[:, s : s + 1], h[:], mybir.AxisListType.X, ALU.max, negate=True
+            )
+            look = held([P, M], F32, "cooled%d" % s)
+            nc.scalar.activation(
+                out=look[:], in_=h[:].indirect(pos1_t[:]), func=ACT.Exp, bias=neg_top[:, s : s + 1]
+            )
+            cooled.append(look)
+
+        for t in range(PACK):
+            s = PACK + t
+            nc.vector.scalar_tensor_tensor(
+                lat[1][:, t, :], anti[s][:], mix_c[:, s : s + 1], lat[1][:, t, :], ALU.mult, ALU.add
+            )
+        w3_q = [quantise(w3_rounded[b], "w3_q%d" % b) for b in range(H // PASS)]
+
+        z = keep.tile([P, SLICES, M], F32, name="z", tag="top_then_log", align_bytes=64)
+        z_b = [held([P, M, PACK], BF16, "z_b%d" % b, "w1_b%d0" % b) for b in range(H // PASS)]
+        z_w = [held([P, M], U32, "z_w%d" % b) for b in range(H // PASS)]
+        z_s = [held([P, M], U8, "z_s%d" % b) for b in range(H // PASS)]
+        y_acc = [psum.tile([P, PACK, QUARTER], F32, name="y_acc", tag="acc") for k in range(M // QUARTER)]
+        y = held([P, PACK, M], F32, "y")
+        y_b = held([P, M, PACK], BF16, "y_b", "w1_b01")
+        y_w = held([P, M], U32, "y_w")
+        y_s = held([P, M], U8, "y_s")
+
+        def make_z(b, cols):
+            for t in range(PACK):
+                s = PACK * b + t
+                nc.scalar.activation(
+                    out=z[:, s, cols], in_=cooled[s][:, cols], func=ACT.Ln, bias=base_c[:, s : s + 1]
+                )
+                nc.vector.scalar_tensor_tensor(
+                    z[:, s, cols], z[:, s, cols], mix_c[:, s : s + 1], lat[b][:, t, cols],
+                    ALU.mult, ALU.add,
+                )
+
+        def interleave(copy, dst, src, cols):
+            copy(
+                out=dst[:, cols, :].rearrange("p (c i) t -> p c t i", i=4),
+                in_=src[:, :, cols].rearrange("p t (c i) -> p c t i", i=4),
+            )
+
+        def quantise_cols(words, scales, src, cols):
+            nc.vector.quantize_mx(
+                out=words[:, cols].bitcast(FP8X4),
+                scales=scales[:, cols],
+                in_=src[:, cols, :].rearrange("p m t -> p (m t)"),
+            )
+
+        def second_stage(b, k):
+            cols = slice(k * QUARTER, (k + 1) * QUARTER)
+            for t in range(PACK):
+                nc.tensor.matmul_mx(
+                    out=y_acc[k][:, t, :],
+                    lhsT=w3_q[b][0][:, P * t : P * (t + 1)].bitcast(FP8X4),
+                    lhsT_scale=w3_q[b][1][:, P * t : P * (t + 1)],
+                    rhs=z_w[b][:, cols].bitcast(FP8X4),
+                    rhs_scale=z_s[b][:, cols],
+                    start=(b == 0 and t == 0),
+                    stop=(b == 1 and t == PACK - 1),
+                )
+
+        whole = slice(0, M)
+        make_z(0, whole)
+        interleave(nc.vector.tensor_copy, z_b[0], z[:, 0:PACK, :], whole)
+        quantise_cols(z_w[0], z_s[0], z_b[0], whole)
+        for k in range(M // QUARTER):
+            second_stage(0, k)
+
+        out_rows = out_0.rearrange("(p t) m -> p t m", t=PACK)
+        out_words = out_1[0].rearrange("p m t -> p (m t)").bitcast(I32)
+        for half in range(2):
+            cols = slice(half * M // 2, (half + 1) * M // 2)
+            make_z(1, cols)
+            interleave(nc.scalar.copy, z_b[1], z[:, PACK : 2 * PACK, :], cols)
+            quantise_cols(z_w[1], z_s[1], z_b[1], cols)
+            for k in range(2 * half, 2 * half + 2):
+                second_stage(1, k)
+        for half in range(2):
+            cols = slice(half * M // 2, (half + 1) * M // 2)
+            for k in range(2 * half, 2 * half + 2):
+                nc.scalar.copy(out=y[:, :, k * QUARTER : (k + 1) * QUARTER], in_=y_acc[k][:])
+            nc.sync.dma_start(out=out_rows[:, :, cols], in_=y[:, :, cols])
+            interleave(nc.vector.tensor_copy, y_b, y, cols)
+            quantise_cols(y_w, y_s, y_b, cols)
+            nc.sync.dma_start(out=out_words[:, cols], in_=y_w[:, cols].bitcast(I32))
+        for q in range(4):
+            queue = nc.sync if q % 2 == 0 else nc.scalar
+            queue.dma_start(
+                out=out_2[0, 4 * q : 4 * q + 4, :].bitcast(I32),
+                in_=y_s[32 * q : 32 * q + 4, :].bitcast(I32),
+            )

@@ -25,6 +25,8 @@ PASSES = K // PASS
 SLICES = H // P
 HALVES = S // BANK
 QUARTER = 128
+RUN = 4
+G_ON_VECTOR = 6
 
 
 def tile_list_polymorph_well_features_kernel(
@@ -82,17 +84,13 @@ def tile_list_polymorph_well_features_kernel(
                 in_=w2_scales[:, 4 * q : 4 * q + 4, :].rearrange("a r e -> r a e").bitcast(I32),
             )
 
-        def load_rows(vec, name):
-            cols = held([P, SLICES], F32, name)
-            nc.sync.dma_start(
-                out=cols[:].rearrange("p (b t) -> p b t", t=PACK),
-                in_=vec.rearrange("(b p t) -> p b t", p=P, t=PACK),
-            )
-            return cols
+        def load_dealt_rows(src, b, dst):
+            rows = src[b * PASS : (b + 1) * PASS, :].rearrange("(g t j) m -> t g j m", t=PACK, j=RUN)
+            for t in range(PACK):
+                nc.sync.dma_start(out=dst[:, t, :], in_=rows[t])
 
-        def load_weight(w, a, b, chunk=None):
-            if chunk is None:
-                chunk = raw.tile([P, PACK, PASS], F32, name="w_raw", tag="w_raw")
+        def load_weight(w, a, b):
+            chunk = raw.tile([P, PACK, PASS], F32, name="w_raw", tag="w_raw")
             nc.sync.dma_start(
                 out=chunk[:],
                 in_=w[a * PASS : (a + 1) * PASS, b * PASS : (b + 1) * PASS].rearrange(
@@ -104,14 +102,13 @@ def tile_list_polymorph_well_features_kernel(
         w1_raw = {}
         w1_raw[0, 0] = load_weight(w1, 0, 0)
         nc.sync.dma_start(pos2_t[:], pos2)
-        temp_c = load_rows(temp, "temp_c")
-        shift_c = load_rows(shift, "shift_c")
+        vec_raw = held([4, H], F32, "vec_raw")
+        for v, vec in enumerate((temp, shift, mix, base)):
+            nc.sync.dma_start(out=vec_raw[v : v + 1, :], in_=vec.rearrange("(o r) -> o r", o=1))
         w1_raw[1, 0] = load_weight(w1, 1, 0)
         w1_raw[0, 1] = load_weight(w1, 0, 1)
         w1_raw[1, 1] = load_weight(w1, 1, 1)
         nc.sync.dma_start(pos1_t[:], pos1)
-        mix_c = load_rows(mix, "mix_c")
-        base_c = load_rows(base, "base_c")
 
         blank_all = held([P, S], F32, "blank_all")
         per_part = S // P
@@ -138,8 +135,8 @@ def tile_list_polymorph_well_features_kernel(
         for a in range(PASSES):
             dealt = held([P, 2 * H], U8, "w2_w%d" % a)
             nc.scalar.copy(
-                out=dealt[:].bitcast(U16).rearrange("p (b t c i) -> p b c t i", t=PACK, c=16, i=8),
-                in_=w2_raw[:, a, :].bitcast(U16).rearrange("p (b c i t) -> p b c t i", t=PACK, c=16, i=8),
+                out=dealt[:].bitcast(U32).rearrange("p (b t g w) -> p b g t w", b=2, t=PACK, w=2),
+                in_=w2_raw[:, a, :].bitcast(U32).rearrange("p (b g t w) -> p b g t w", b=2, t=PACK, w=2),
             )
             w2_w.append(dealt)
 
@@ -156,33 +153,30 @@ def tile_list_polymorph_well_features_kernel(
 
         w2_s = held([P, PASSES, H], U8, "w2_s")
         nc.vector.tensor_copy(
-            out=w2_s[:].rearrange("p a (b t c i) -> p (a b) c t i", t=PACK, c=8, i=16),
-            in_=w2_s_raw[:].rearrange("p a (b c i t) -> p (a b) c t i", t=PACK, c=8, i=16),
+            out=w2_s[:].bitcast(I32).rearrange("p a (b t c i) -> p (a b) c t i", b=2, t=PACK, i=4),
+            in_=w2_s_raw[:].bitcast(I32).rearrange("p a (b c i t) -> p (a b) c t i", b=2, t=PACK, i=4),
         )
-        w3_raw = [
-            load_weight(w3, b, 0, held([P, PACK, N], F32, "w3_raw%d" % b, "tab_w%d" % b))
-            for b in range(H // PASS)
-        ]
-        lat = []
+        lat = [held([P, PACK, M], F32, "lat%d" % b) for b in range(H // PASS)]
+        w3_raw = [held([P, PACK, N], F32, "w3_raw%d" % b, "tab_w%d" % b) for b in range(H // PASS)]
         for b in range(H // PASS):
-            rows = held([P, PACK, M], F32, "lat%d" % b)
-            nc.sync.dma_start(
-                out=rows[:],
-                in_=lattice[b * PASS : (b + 1) * PASS, :].rearrange("(p t) m -> p t m", t=PACK),
-            )
-            lat.append(rows)
+            load_dealt_rows(lattice, b, lat[b])
+        for b in range(H // PASS):
+            load_dealt_rows(w3, b, w3_raw[b])
 
-        def round_weight(engine, chunk, name, pieces):
-            rounded = held([P, PACK, P, PACK], BF16, name)
-            step = P // pieces
-            for k in range(pieces):
-                dst = rounded[:, :, k * step : (k + 1) * step, :].rearrange("p t c i -> p c t i")
-                src = chunk[:].rearrange("p i (c t) -> p c t i", t=PACK)[:, k * step : (k + 1) * step, :, :]
-                if engine == "scalar":
-                    nc.scalar.copy(out=dst, in_=src)
-                else:
-                    nc.gpsimd.tensor_scalar(dst, src, 1.0, 0.0, ALU.mult, ALU.add)
-            return rounded
+        vec_dealt = held([P, H], F32, "vec_dealt")
+        nc.gpsimd.memset(vec_dealt[:], 0.0)
+        nc.scalar.copy(
+            out=vec_dealt[0:4, :].rearrange("v (b t g j) -> v b g t j", b=2, t=PACK, j=RUN),
+            in_=vec_raw[:].rearrange("v (b g t j) -> v b g t j", b=2, t=PACK, j=RUN),
+        )
+        per_row = held([P, SLICES, 4], F32, "per_row")
+        for b in range(H // PASS):
+            turned = psum.tile([P, PACK, P], F32, name="turned", tag="acc")
+            for t in range(PACK):
+                s = PACK * b + t
+                nc.tensor.transpose(turned[:, t, :], vec_dealt[:, P * s : P * (s + 1)], ident[:])
+            nc.scalar.copy(out=per_row[:, PACK * b : PACK * (b + 1), :], in_=turned[:, :, 0:4])
+        temp_c, shift_c, mix_c, base_c = [per_row[:, :, v] for v in range(4)]
 
         def quantise(rounded, name):
             words = held([P, PASS], U32, name + "_w")
@@ -190,17 +184,21 @@ def tile_list_polymorph_well_features_kernel(
             nc.vector.quantize_mx(
                 out=words[:].bitcast(FP8X4),
                 scales=scales[:],
-                in_=rounded[:].rearrange("p t c i -> p (t c i)"),
+                in_=rounded.rearrange("p t c i -> p (t c i)"),
             )
             return words, scales
 
         w1_q = {}
         for b in range(H // PASS):
             for a in range(PASSES):
-                rounded = round_weight("scalar", w1_raw[a, b], "w1_b%d%d" % (a, b), 1)
-                w1_q[a, b] = quantise(rounded, "w1_q%d%d" % (a, b))
+                rounded = held([P, PACK, P, PACK], BF16, "w1_b%d%d" % (a, b))
+                nc.scalar.copy(
+                    out=rounded[:].rearrange("p t (g j) i -> p g t i j", j=RUN),
+                    in_=w1_raw[a, b][:].rearrange("p i (g t j) -> p g t i j", t=PACK, j=RUN),
+                )
+                w1_q[a, b] = quantise(rounded[:], "w1_q%d%d" % (a, b))
 
-        def score(stationary):
+        def score(stationary, on_vector):
             rows = scores.tile([P, S], F32, name="rows", tag="rows")
             for half in range(HALVES):
                 cols = slice(half * BANK, (half + 1) * BANK)
@@ -216,28 +214,32 @@ def tile_list_polymorph_well_features_kernel(
                         start=(a == 0),
                         stop=(a == PASSES - 1),
                     )
-                nc.vector.tensor_tensor(rows[:, cols], acc[:], blank_all[:, cols], ALU.subtract)
+                if on_vector:
+                    nc.vector.tensor_tensor(rows[:, cols], acc[:], blank_all[:, cols], ALU.subtract)
+                else:
+                    nc.scalar.copy(out=rows[:, cols], in_=acc[:])
+                    nc.gpsimd.tensor_tensor(rows[:, cols], rows[:, cols], blank_all[:, cols], ALU.subtract)
             return rows
 
-        anti = []
-        for s in range(SLICES):
-            g = score(
+        g_rows = [
+            score(
                 lambda a: (
                     w2_w[a][:, 2 * P * s : 2 * P * (s + 1)].bitcast(FP4X4),
                     w2_s[:, a, P * s : P * (s + 1)],
-                )
+                ),
+                s < G_ON_VECTOR,
             )
+            for s in range(SLICES)
+        ]
+        for s in range(SLICES):
+            b, t = divmod(s, PACK)
             c = held([P, M], F32, "anti%d" % s)
             nc.scalar.activation(
-                out=c[:], in_=g[:].indirect(pos2_t[:]), func=ACT.Exp,
+                out=c[:], in_=g_rows[s][:].indirect(pos2_t[:]), func=ACT.Exp,
                 bias=shift_c[:, s : s + 1], scale=temp_c[:, s : s + 1],
             )
-            anti.append(c)
-
-        w3_rounded = [round_weight("gpsimd", w3_raw[b], "w3_b%d" % b, 2) for b in range(H // PASS)]
-        for t in range(PACK):
-            nc.gpsimd.tensor_scalar(anti[t][:], anti[t][:], mix_c[:, t : t + 1], 0.0, ALU.mult, ALU.add)
-            nc.gpsimd.tensor_tensor(lat[0][:, t, :], lat[0][:, t, :], anti[t][:], ALU.add)
+            nc.gpsimd.tensor_scalar(c[:], c[:], mix_c[:, s : s + 1], 0.0, ALU.mult, ALU.add)
+            nc.gpsimd.tensor_tensor(lat[b][:, t, :], lat[b][:, t, :], c[:], ALU.add)
 
         neg_top = keep.tile([P, SLICES], F32, name="neg_top", tag="top_then_log", align_bytes=64)
         cooled = []
@@ -247,7 +249,8 @@ def tile_list_polymorph_well_features_kernel(
                 lambda a: (
                     w1_q[a, b][0][:, P * t : P * (t + 1)].bitcast(FP8X4),
                     w1_q[a, b][1][:, P * t : P * (t + 1)],
-                )
+                ),
+                True,
             )
             nc.vector.tensor_reduce(
                 neg_top[:, s : s + 1], h[:], mybir.AxisListType.X, ALU.max, negate=True
@@ -258,12 +261,16 @@ def tile_list_polymorph_well_features_kernel(
             )
             cooled.append(look)
 
-        for t in range(PACK):
-            s = PACK + t
-            nc.vector.scalar_tensor_tensor(
-                lat[1][:, t, :], anti[s][:], mix_c[:, s : s + 1], lat[1][:, t, :], ALU.mult, ALU.add
-            )
-        w3_q = [quantise(w3_rounded[b], "w3_q%d" % b) for b in range(H // PASS)]
+        w3_b = held([P, H // PASS, PACK, P, PACK], BF16, "w3_b", "blank_all")
+        w3_q = []
+        step = P // 4
+        for b in range(H // PASS):
+            for k in range(4):
+                nc.vector.tensor_copy(
+                    out=w3_b[:, b, :, k * step : (k + 1) * step, :].rearrange("p t c i -> p c t i"),
+                    in_=w3_raw[b][:].rearrange("p i (c t) -> p c t i", t=PACK)[:, k * step : (k + 1) * step, :, :],
+                )
+            w3_q.append(quantise(w3_b[:, b, :, :, :], "w3_q%d" % b))
 
         z = keep.tile([P, SLICES, M], F32, name="z", tag="top_then_log", align_bytes=64)
         z_b = [held([P, M, PACK], BF16, "z_b%d" % b, "w1_b%d0" % b) for b in range(H // PASS)]
@@ -324,7 +331,7 @@ def tile_list_polymorph_well_features_kernel(
         for half in range(2):
             cols = slice(half * M // 2, (half + 1) * M // 2)
             make_z(1, cols)
-            interleave(nc.scalar.copy, z_b[1], z[:, PACK : 2 * PACK, :], cols)
+            interleave(nc.scalar.copy if half == 0 else nc.vector.tensor_copy, z_b[1], z[:, PACK : 2 * PACK, :], cols)
             quantise_cols(z_w[1], z_s[1], z_b[1], cols)
             for k in range(2 * half, 2 * half + 2):
                 second_stage(1, k)

@@ -48,10 +48,9 @@ def tile_list_polymorph_well_features_kernel(
         pos1_t = lists.tile([P, M // 16], U16, name="pos1_t")
         pos2_t = lists.tile([P, M // 16], U16, name="pos2_t")
 
-        tab_s = held([P, PASSES, T], U8, "tab_s")
+        tab_s = held([P, T], U8, "tab_s")
         w2_s_raw = held([P, PASSES, H], U8, "w2_s_raw")
-        nc.gpsimd.memset(tab_s[:, 0, :].bitcast(I32), 0)
-        nc.vector.memset(tab_s[:, 1, :].bitcast(I32), 0)
+        nc.gpsimd.memset(tab_s[:].bitcast(I32), 0)
         nc.vector.memset(w2_s_raw[:].bitcast(I32), 0)
         ident = held([P, P], F32, "ident")
         make_identity(nc, ident[:])
@@ -70,8 +69,8 @@ def tile_list_polymorph_well_features_kernel(
         load_table_words(0)
         for q in range(4):
             nc.scalar.dma_start(
-                out=tab_s[32 * q : 32 * q + 4, :, :].bitcast(I32),
-                in_=tab_scales[:, 4 * q : 4 * q + 4, :].rearrange("a r e -> r a e").bitcast(I32),
+                out=tab_s[32 * q : 32 * q + 4 * PASSES, :].bitcast(I32),
+                in_=tab_scales[:, 4 * q : 4 * q + 4, :].bitcast(I32),
             )
         load_table_words(1)
         w2_raw = held([P, PASSES, 2 * H], U8, "w2_raw")
@@ -125,11 +124,10 @@ def tile_list_polymorph_well_features_kernel(
                 func=ACT.Copy,
             )
 
-        v_s = []
-        for a in range(PASSES):
-            picked = held([P, S], U8, "v_s%d" % a)
-            nc.vector.tensor_copy(picked[:], tab_s[:, a, :].indirect(offs_t[:]))
-            v_s.append(picked)
+        v_s = [held([P, S], U8, "v_s%d" % a) for a in range(PASSES)]
+        nc.vector.memset(v_s[1][:].bitcast(I32), 0)
+        nc.vector.tensor_copy(v_s[0][:], tab_s[:].indirect(offs_t[:]))
+        nc.gpsimd.dma_start(out=v_s[1][0:112, :].bitcast(I32), in_=v_s[0][4:116, :].bitcast(I32))
 
         w2_w = []
         for a in range(PASSES):
@@ -165,7 +163,7 @@ def tile_list_polymorph_well_features_kernel(
 
         vec_dealt = held([P, H], F32, "vec_dealt")
         nc.gpsimd.memset(vec_dealt[:], 0.0)
-        nc.scalar.copy(
+        nc.gpsimd.tensor_copy(
             out=vec_dealt[0:4, :].rearrange("v (b t g j) -> v b g t j", b=2, t=PACK, j=RUN),
             in_=vec_raw[:].rearrange("v (b g t j) -> v b g t j", b=2, t=PACK, j=RUN),
         )
@@ -328,21 +326,24 @@ def tile_list_polymorph_well_features_kernel(
 
         out_rows = out_0.rearrange("(p t) m -> p t m", t=PACK)
         out_words = out_1[0].rearrange("p m t -> p (m t)").bitcast(I32)
-        for half in range(2):
-            cols = slice(half * M // 2, (half + 1) * M // 2)
+        halves = [slice(half * M // 2, (half + 1) * M // 2) for half in range(2)]
+        for cols in halves:
             make_z(1, cols)
-            interleave(nc.scalar.copy if half == 0 else nc.vector.tensor_copy, z_b[1], z[:, PACK : 2 * PACK, :], cols)
+        interleave(nc.scalar.copy, z_b[1], z[:, PACK : 2 * PACK, :], halves[0])
+        interleave(nc.vector.tensor_copy, z_b[1], z[:, PACK : 2 * PACK, :], halves[1])
+        for half, cols in enumerate(halves):
             quantise_cols(z_w[1], z_s[1], z_b[1], cols)
             for k in range(2 * half, 2 * half + 2):
                 second_stage(1, k)
-        for half in range(2):
-            cols = slice(half * M // 2, (half + 1) * M // 2)
-            for k in range(2 * half, 2 * half + 2):
-                nc.scalar.copy(out=y[:, :, k * QUARTER : (k + 1) * QUARTER], in_=y_acc[k][:])
-            nc.sync.dma_start(out=out_rows[:, :, cols], in_=y[:, :, cols])
+        for k in range(M // QUARTER):
+            cols = slice(k * QUARTER, (k + 1) * QUARTER)
+            nc.scalar.copy(out=y[:, :, cols], in_=y_acc[k][:])
             interleave(nc.vector.tensor_copy, y_b, y, cols)
             quantise_cols(y_w, y_s, y_b, cols)
-            nc.sync.dma_start(out=out_words[:, cols], in_=y_w[:, cols].bitcast(I32))
+            if k % 2 == 1:
+                cols = halves[k // 2]
+                nc.scalar.dma_start(out=out_rows[:, :, cols], in_=y[:, :, cols])
+                nc.sync.dma_start(out=out_words[:, cols], in_=y_w[:, cols].bitcast(I32))
         for q in range(4):
             queue = nc.sync if q % 2 == 0 else nc.scalar
             queue.dma_start(

from contextlib import ExitStack

import concourse.mybir as mybir
from concourse.masks import make_identity

K, H, N, T, S, M = 1024, 1024, 512, 2048, 1024, 512
FLOPS = 2 * K * H * S * 2 + 2 * H * N * M

F32 = mybir.dt.float32
BF16 = mybir.dt.bfloat16
I32 = mybir.dt.int32
U32 = mybir.dt.uint32
U16 = mybir.dt.uint16
U8 = mybir.dt.uint8
FP8X4 = mybir.dt.float8_e4m3fn_x4
FP4X4 = mybir.dt.float4_e2m1fn_x4
ACT = mybir.ActivationFunctionType
ALU = mybir.AluOpType

P = 128
PACK = 4
PASS = P * PACK
BANK = 512
PASSES = K // PASS
SLICES = H // P
HALVES = S // BANK
QUARTER = 128
RUN = 4
G_ON_VECTOR = 6


def tile_list_polymorph_well_features_kernel(
    tc, tab_words, tab_scales, offs, pos1, pos2, w1, w2_words, w2_scales,
    blank, temp, shift, base, mix, lattice, w3, out_0, out_1, out_2,
):
    nc = tc.nc
    with ExitStack() as ctx:
        lists = ctx.enter_context(tc.tile_pool(name="lists", bufs=1))
        keep = ctx.enter_context(tc.tile_pool(name="keep", bufs=1))
        raw = ctx.enter_context(tc.tile_pool(name="raw", bufs=4))
        scores = ctx.enter_context(tc.tile_pool(name="scores", bufs=8))
        psum = ctx.enter_context(tc.psum_pool(name="psum", bufs=8))

        def held(shape, dtype, name, tag=""):
            return keep.tile(shape, dtype, name=name, tag=tag or name, align_bytes=64)

        offs_t = lists.tile([P, S // 16], U16, name="offs_t")
        pos1_t = lists.tile([P, M // 16], U16, name="pos1_t")
        pos2_t = lists.tile([P, M // 16], U16, name="pos2_t")

        tab_s = held([P, T], U8, "tab_s")
        w2_s_raw = held([P, PASSES, H], U8, "w2_s_raw")
        nc.gpsimd.memset(tab_s[:].bitcast(I32), 0)
        nc.vector.memset(w2_s_raw[:].bitcast(I32), 0)
        ident = held([P, P], F32, "ident")
        make_identity(nc, ident[:])

        nc.sync.dma_start(offs_t[:], offs)
        blank_col = held([P, S // P], F32, "blank_col")
        nc.sync.dma_start(out=blank_col[:], in_=blank.rearrange("(p c) -> p c", p=P))
        tab_w = [held([P, T], U32, "tab_w%d" % a) for a in range(PASSES)]

        def load_table_words(a):
            nc.sync.dma_start(
                out=tab_w[a][:].bitcast(I32),
                in_=tab_words[a].rearrange("p n t -> p (n t)").bitcast(I32),
            )

        load_table_words(0)
        for q in range(4):
            nc.scalar.dma_start(
                out=tab_s[32 * q : 32 * q + 4 * PASSES, :].bitcast(I32),
                in_=tab_scales[:, 4 * q : 4 * q + 4, :].bitcast(I32),
            )
        load_table_words(1)
        w2_raw = held([P, PASSES, 2 * H], U8, "w2_raw")
        nc.sync.dma_start(
            out=w2_raw[:].bitcast(I32), in_=w2_words.rearrange("a p e -> p a e").bitcast(I32)
        )
        for q in range(4):
            nc.sync.dma_start(
                out=w2_s_raw[32 * q : 32 * q + 4, :, :].bitcast(I32),
                in_=w2_scales[:, 4 * q : 4 * q + 4, :].rearrange("a r e -> r a e").bitcast(I32),
            )

        def load_dealt_rows(src, b, dst):
            rows = src[b * PASS : (b + 1) * PASS, :].rearrange("(g t j) m -> t g j m", t=PACK, j=RUN)
            for t in range(PACK):
                nc.sync.dma_start(out=dst[:, t, :], in_=rows[t])

        def load_weight(w, a, b):
            chunk = raw.tile([P, PACK, PASS], F32, name="w_raw", tag="w_raw")
            nc.sync.dma_start(
                out=chunk[:],
                in_=w[a * PASS : (a + 1) * PASS, b * PASS : (b + 1) * PASS].rearrange(
                    "(p i) c -> p i c", i=PACK
                ),
            )
            return chunk

        w1_raw = {}
        w1_raw[0, 0] = load_weight(w1, 0, 0)
        nc.sync.dma_start(pos2_t[:], pos2)
        vec_raw = held([4, H], F32, "vec_raw")
        for v, vec in enumerate((temp, shift, mix, base)):
            nc.sync.dma_start(out=vec_raw[v : v + 1, :], in_=vec.rearrange("(o r) -> o r", o=1))
        w1_raw[1, 0] = load_weight(w1, 1, 0)
        w1_raw[0, 1] = load_weight(w1, 0, 1)
        w1_raw[1, 1] = load_weight(w1, 1, 1)
        nc.sync.dma_start(pos1_t[:], pos1)

        blank_all = held([P, S], F32, "blank_all")
        per_part = S // P
        for half in range(per_part // 4):
            spread = psum.tile([P, 4, P], F32, name="spread", tag="acc")
            for c in range(4):
                col = 4 * half + c
                nc.tensor.transpose(
                    spread[:, c, :], blank_col[:, col : col + 1].to_broadcast([P, P]), ident[:]
                )
            nc.scalar.activation(
                out=blank_all[:].rearrange("p (n c) -> p n c", c=per_part)[:, :, 4 * half : 4 * half + 4],
                in_=spread[:].rearrange("p c n -> p n c"),
                func=ACT.Copy,
            )

        v_s = [held([P, S], U8, "v_s%d" % a) for a in range(PASSES)]
        nc.vector.memset(v_s[1][:].bitcast(I32), 0)
        nc.vector.tensor_copy(v_s[0][:], tab_s[:].indirect(offs_t[:]))
        nc.gpsimd.dma_start(out=v_s[1][0:112, :].bitcast(I32), in_=v_s[0][4:116, :].bitcast(I32))

        w2_w = []
        for a in range(PASSES):
            dealt = held([P, 2 * H], U8, "w2_w%d" % a)
            nc.scalar.copy(
                out=dealt[:].bitcast(U32).rearrange("p (b t g w) -> p b g t w", b=2, t=PACK, w=2),
                in_=w2_raw[:, a, :].bitcast(U32).rearrange("p (b g t w) -> p b g t w", b=2, t=PACK, w=2),
            )
            w2_w.append(dealt)

        v_w = {}
        cols_per_half = BANK // 16
        for a in range(PASSES):
            for half in range(HALVES):
                picked = held([P, BANK], U32, "v_w%d%d" % (a, half))
                nc.vector.tensor_copy(
                    picked[:],
                    tab_w[a][:].indirect(offs_t[:, half * cols_per_half : (half + 1) * cols_per_half]),
                )
                v_w[a, half] = picked

        w2_s = held([P, PASSES, H], U8, "w2_s")
        nc.vector.tensor_copy(
            out=w2_s[:].bitcast(I32).rearrange("p a (b t c i) -> p (a b) c t i", b=2, t=PACK, i=4),
            in_=w2_s_raw[:].bitcast(I32).rearrange("p a (b c i t) -> p (a b) c t i", b=2, t=PACK, i=4),
        )
        lat = [held([P, PACK, M], F32, "lat%d" % b) for b in range(H // PASS)]
        w3_raw = [held([P, PACK, N], F32, "w3_raw%d" % b, "tab_w%d" % b) for b in range(H // PASS)]
        for b in range(H // PASS):
            load_dealt_rows(lattice, b, lat[b])
        for b in range(H // PASS):
            load_dealt_rows(w3, b, w3_raw[b])

        vec_dealt = held([P, H], F32, "vec_dealt")
        nc.gpsimd.memset(vec_dealt[:], 0.0)
        nc.gpsimd.tensor_copy(
            out=vec_dealt[0:4, :].rearrange("v (b t g j) -> v b g t j", b=2, t=PACK, j=RUN),
            in_=vec_raw[:].rearrange("v (b g t j) -> v b g t j", b=2, t=PACK, j=RUN),
        )
        per_row = held([P, SLICES, 4], F32, "per_row")
        for b in range(H // PASS):
            turned = psum.tile([P, PACK, P], F32, name="turned", tag="acc")
            for t in range(PACK):
                s = PACK * b + t
                nc.tensor.transpose(turned[:, t, :], vec_dealt[:, P * s : P * (s + 1)], ident[:])
            nc.scalar.copy(out=per_row[:, PACK * b : PACK * (b + 1), :], in_=turned[:, :, 0:4])
        temp_c, shift_c, mix_c, base_c = [per_row[:, :, v] for v in range(4)]

        def quantise(rounded, name):
            words = held([P, PASS], U32, name + "_w")
            scales = held([P, PASS], U8, name + "_s")
            nc.vector.quantize_mx(
                out=words[:].bitcast(FP8X4),
                scales=scales[:],
                in_=rounded.rearrange("p t c i -> p (t c i)"),
            )
            return words, scales

        w1_q = {}
        for b in range(H // PASS):
            for a in range(PASSES):
                rounded = held([P, PACK, P, PACK], BF16, "w1_b%d%d" % (a, b))
                nc.scalar.copy(
                    out=rounded[:].rearrange("p t (g j) i -> p g t i j", j=RUN),
                    in_=w1_raw[a, b][:].rearrange("p i (g t j) -> p g t i j", t=PACK, j=RUN),
                )
                w1_q[a, b] = quantise(rounded[:], "w1_q%d%d" % (a, b))

        def score(stationary, on_vector):
            rows = scores.tile([P, S], F32, name="rows", tag="rows")
            for half in range(HALVES):
                cols = slice(half * BANK, (half + 1) * BANK)
                acc = psum.tile([P, BANK], F32, name="acc", tag="acc")
                for a in range(PASSES):
                    words, scales = stationary(a)
                    nc.tensor.matmul_mx(
                        out=acc[:],
                        lhsT=words,
                        lhsT_scale=scales,
                        rhs=v_w[a, half][:].bitcast(FP8X4),
                        rhs_scale=v_s[a][:, cols],
                        start=(a == 0),
                        stop=(a == PASSES - 1),
                    )
                if on_vector:
                    nc.vector.tensor_tensor(rows[:, cols], acc[:], blank_all[:, cols], ALU.subtract)
                else:
                    nc.scalar.copy(out=rows[:, cols], in_=acc[:])
                    nc.gpsimd.tensor_tensor(rows[:, cols], rows[:, cols], blank_all[:, cols], ALU.subtract)
            return rows

        g_rows = [
            score(
                lambda a: (
                    w2_w[a][:, 2 * P * s : 2 * P * (s + 1)].bitcast(FP4X4),
                    w2_s[:, a, P * s : P * (s + 1)],
                ),
                s < G_ON_VECTOR,
            )
            for s in range(SLICES)
        ]
        for s in range(SLICES):
            b, t = divmod(s, PACK)
            c = held([P, M], F32, "anti%d" % s)
            nc.scalar.activation(
                out=c[:], in_=g_rows[s][:].indirect(pos2_t[:]), func=ACT.Exp,
                bias=shift_c[:, s : s + 1], scale=temp_c[:, s : s + 1],
            )
            nc.gpsimd.tensor_scalar(c[:], c[:], mix_c[:, s : s + 1], 0.0, ALU.mult, ALU.add)
            nc.gpsimd.tensor_tensor(lat[b][:, t, :], lat[b][:, t, :], c[:], ALU.add)

        neg_top = keep.tile([P, SLICES], F32, name="neg_top", tag="top_then_log", align_bytes=64)
        cooled = []
        for s in range(SLICES):
            b, t = divmod(s, PACK)
            h = score(
                lambda a: (
                    w1_q[a, b][0][:, P * t : P * (t + 1)].bitcast(FP8X4),
                    w1_q[a, b][1][:, P * t : P * (t + 1)],
                ),
                True,
            )
            nc.vector.tensor_reduce(
                neg_top[:, s : s + 1], h[:], mybir.AxisListType.X, ALU.max, negate=True
            )
            look = held([P, M], F32, "cooled%d" % s)
            nc.scalar.activation(
                out=look[:], in_=h[:].indirect(pos1_t[:]), func=ACT.Exp, bias=neg_top[:, s : s + 1]
            )
            cooled.append(look)

        w3_b = held([P, H // PASS, PACK, P, PACK], BF16, "w3_b", "blank_all")
        w3_q = []
        step = P // 4
        for b in range(H // PASS):
            for k in range(4):
                nc.vector.tensor_copy(
                    out=w3_b[:, b, :, k * step : (k + 1) * step, :].rearrange("p t c i -> p c t i"),
                    in_=w3_raw[b][:].rearrange("p i (c t) -> p c t i", t=PACK)[:, k * step : (k + 1) * step, :, :],
                )
            w3_q.append(quantise(w3_b[:, b, :, :, :], "w3_q%d" % b))

        z = keep.tile([P, SLICES, M], F32, name="z", tag="top_then_log", align_bytes=64)
        z_b = [held([P, M, PACK], BF16, "z_b%d" % b, "w1_b%d0" % b) for b in range(H // PASS)]
        z_w = [held([P, M], U32, "z_w%d" % b) for b in range(H // PASS)]
        z_s = [held([P, M], U8, "z_s%d" % b) for b in range(H // PASS)]
        y_acc = [psum.tile([P, PACK, QUARTER], F32, name="y_acc", tag="acc") for k in range(M // QUARTER)]
        y = held([P, PACK, M], F32, "y")
        y_b = held([P, M, PACK], BF16, "y_b", "w1_b01")
        y_w = held([P, M], U32, "y_w")
        y_s = held([P, M], U8, "y_s")

        def make_z(b, cols):
            for t in range(PACK):
                s = PACK * b + t
                nc.scalar.activation(
                    out=z[:, s, cols], in_=cooled[s][:, cols], func=ACT.Ln, bias=base_c[:, s : s + 1]
                )
                nc.vector.scalar_tensor_tensor(
                    z[:, s, cols], z[:, s, cols], mix_c[:, s : s + 1], lat[b][:, t, cols],
                    ALU.mult, ALU.add,
                )

        def interleave(copy, dst, src, cols):
            copy(
                out=dst[:, cols, :].rearrange("p (c i) t -> p c t i", i=4),
                in_=src[:, :, cols].rearrange("p t (c i) -> p c t i", i=4),
            )

        def quantise_cols(words, scales, src, cols):
            nc.vector.quantize_mx(
                out=words[:, cols].bitcast(FP8X4),
                scales=scales[:, cols],
                in_=src[:, cols, :].rearrange("p m t -> p (m t)"),
            )

        def second_stage(b, k):
            cols = slice(k * QUARTER, (k + 1) * QUARTER)
            for t in range(PACK):
                nc.tensor.matmul_mx(
                    out=y_acc[k][:, t, :],
                    lhsT=w3_q[b][0][:, P * t : P * (t + 1)].bitcast(FP8X4),
                    lhsT_scale=w3_q[b][1][:, P * t : P * (t + 1)],
                    rhs=z_w[b][:, cols].bitcast(FP8X4),
                    rhs_scale=z_s[b][:, cols],
                    start=(b == 0 and t == 0),
                    stop=(b == 1 and t == PACK - 1),
                )

        whole = slice(0, M)
        make_z(0, whole)
        interleave(nc.vector.tensor_copy, z_b[0], z[:, 0:PACK, :], whole)
        quantise_cols(z_w[0], z_s[0], z_b[0], whole)
        for k in range(M // QUARTER):
            second_stage(0, k)

        out_rows = out_0.rearrange("(p t) m -> p t m", t=PACK)
        out_words = out_1[0].rearrange("p m t -> p (m t)").bitcast(I32)
        halves = [slice(half * M // 2, (half + 1) * M // 2) for half in range(2)]
        for cols in halves:
            make_z(1, cols)
        interleave(nc.scalar.copy, z_b[1], z[:, PACK : 2 * PACK, :], halves[0])
        interleave(nc.vector.tensor_copy, z_b[1], z[:, PACK : 2 * PACK, :], halves[1])
        for half, cols in enumerate(halves):
            quantise_cols(z_w[1], z_s[1], z_b[1], cols)
            for k in range(2 * half, 2 * half + 2):
                second_stage(1, k)
        for k in range(M // QUARTER):
            cols = slice(k * QUARTER, (k + 1) * QUARTER)
            nc.scalar.copy(out=y[:, :, cols], in_=y_acc[k][:])
            interleave(nc.vector.tensor_copy, y_b, y, cols)
            quantise_cols(y_w, y_s, y_b, cols)
            if k % 2 == 1:
                cols = halves[k // 2]
                nc.scalar.dma_start(out=out_rows[:, :, cols], in_=y[:, :, cols])
                nc.sync.dma_start(out=out_words[:, cols], in_=y_w[:, cols].bitcast(I32))
        for q in range(4):
            queue = nc.sync if q % 2 == 0 else nc.scalar
            queue.dma_start(
                out=out_2[0, 4 * q : 4 * q + 4, :].bitcast(I32),
                in_=y_s[32 * q : 32 * q + 4, :].bitcast(I32),
            )
